import numpy as np
import ml_dtypes


def mxq(x, axis, fmt="e4m3"):
    dtype, down = {"e4m3": (ml_dtypes.float8_e4m3fn, 7), "e5m2": (ml_dtypes.float8_e5m2, 14)}[fmt]
    v = np.moveaxis(np.asarray(x, np.float32).astype(ml_dtypes.bfloat16).astype(np.float64), axis, -1)
    blocks = v.reshape(v.shape[:-1] + (-1, 32))
    amax = np.abs(blocks).max(-1, keepdims=True)
    byte = np.maximum(np.where(amax > 0, np.frexp(amax)[1] - 1 + 127, 0) - down, 1)
    scale = np.exp2(byte - 127.0)
    codes = (blocks / scale).astype(np.float32).astype(dtype).astype(np.float64)
    return np.moveaxis((codes * scale).reshape(v.shape), -1, axis)


WIDE = False


def mx_kscale(k):
    if not WIDE:
        return np.ones(k)
    levels = np.array([10, -10, 5, -5, 0])
    if k % 512:
        return np.exp2(np.random.permutation(np.resize(levels, k // 32))).repeat(32)
    a = np.empty((k // 512, 16))
    for p in range(k // 512):
        a[p, :8] = np.random.permutation(np.resize(levels, 8))
        for g in range(8):
            far = levels[np.abs(levels - a[p, g]) >= 10]
            a[p, g + 8] = far[np.random.randint(len(far))]
    return np.exp2(a.ravel()).repeat(32)


def f64(x):
    return np.asarray(x).astype(np.float64)


def striped(idx):
    return np.tile(idx.reshape(-1, 16).T, (8, 1)).astype(np.uint16)


def unstriped(offs):
    return offs[:16].T.reshape(-1).astype(np.int64)


E2M1 = np.array([0.0, 0.5, 1.0, 1.5, 2.0, 3.0, 4.0, 6.0, -0.0, -0.5, -1.0, -1.5, -2.0, -3.0, -4.0, -6.0])


def pack_weight(w, fmt):
    k, n = w.shape
    w = f64(np.asarray(w, np.float32).astype(ml_dtypes.bfloat16)).reshape(k // 32, 32, n)
    amax = np.abs(w).max(1)
    if fmt == "e4m3":
        byte = np.frexp(amax)[1] - 1 + 127 - 7
    else:
        mant, ex = np.frexp(amax / 6.0)
        byte = np.where(mant > 0.5, ex, ex - 1) + 127
    byte = np.clip(np.where(amax > 0, byte, 1), 1, 254)
    scaled = (w * np.exp2(127.0 - byte)[:, None, :]).reshape(k, n).astype(np.float32)
    by_word = np.ascontiguousarray(scaled.reshape(k // 512, 128, 4, n).transpose(0, 1, 3, 2))
    if fmt == "e4m3":
        words = by_word.astype(ml_dtypes.float8_e4m3fn).view(np.uint8)
    else:
        c = by_word.astype(ml_dtypes.float4_e2m1fn).view(np.uint8) & 0xF
        words = (c[..., 0::2] | (c[..., 1::2] << 4)).reshape(k // 512, 128, 2 * n)
    return np.ascontiguousarray(words), np.ascontiguousarray(byte.astype(np.uint8).reshape(k // 512, 16, n))


def unpack_weight(words, scales, fmt):
    g, _, n = scales.shape
    words = np.ascontiguousarray(words).reshape(g, 128, n, -1)
    if fmt == "e4m3":
        vals = words.view(ml_dtypes.float8_e4m3fn).astype(np.float64)
    else:
        nib = np.empty((g, 128, n, 4), np.uint8)
        nib[..., 0::2] = words & 0xF
        nib[..., 1::2] = words >> 4
        vals = E2M1[nib]
    vals = vals * np.repeat(np.exp2(scales.astype(np.float64) - 127.0), 8, axis=1)[..., None]
    return vals.transpose(0, 1, 3, 2).reshape(g * 512, n)


def planes(y):
    n, m = y.shape
    v = y.astype(np.float32).astype(ml_dtypes.bfloat16).astype(np.float64).reshape(n // 32, 32, m)
    top = np.abs(v).max(1)
    byte = np.clip(np.where(top > 0, np.frexp(top)[1] - 1 + 127 - 7, 1), 1, 254)
    codes = (v * np.exp2(127.0 - byte)[:, None, :]).reshape(n, m).astype(np.float32).astype(ml_dtypes.float8_e4m3fn).view(np.uint8)
    words = codes.reshape(n // 512, 128, 4, m).transpose(0, 1, 3, 2)
    return np.ascontiguousarray(words), np.ascontiguousarray(byte.astype(np.uint8).reshape(n // 512, 16, m))


K, T, G, C1, E, C2, H = 1024, 768, 3, 256, 6, 128, 512
N = 512


def by_expert(wq, xq, E, C):
    return np.concatenate([wq[e].T @ xq[:, e * C:(e + 1) * C] for e in range(E)], axis=1)


def setup_inputs():
    n = np.random.standard_normal
    s = mx_kscale(K)
    u = mx_kscale(H)
    slots1 = np.random.permutation(T)
    slots2 = np.concatenate([q * C1 + np.random.permutation(C1) for q in range(G)])
    x = pack_weight(n((K, T)) * s[:, None], "e4m3")
    wg = [pack_weight(m, "e4m3") for m in n((G, K, H)) / np.sqrt(K) / s[None, :, None] * u]
    we = [pack_weight(m, "e2m1") for m in n((E, H, N)) / np.sqrt(H) / u[None, :, None]]
    return {
        "x_words": x[0],
        "x_scales": x[1],
        "wg_words": np.stack([m[0] for m in wg]),
        "wg_scales": np.stack([m[1] for m in wg]),
        "we_words": np.stack([m[0] for m in we]),
        "we_scales": np.stack([m[1] for m in we]),
        "gate": (np.tile(np.random.uniform(0.2, 1.0, T), (128, 1))).astype(np.float32),
        "offs": striped(slots1),
        "offs2": striped(slots2),
        "dst": striped(slots1[slots2]),
    }


def reference(x_words, x_scales, wg_words, wg_scales, we_words, we_scales, gate, offs, offs2, dst):
    wg = np.stack([unpack_weight(wg_words[e], wg_scales[e], "e4m3") for e in range(G)])
    we = np.stack([unpack_weight(we_words[e], we_scales[e], "e2m1") for e in range(E)])
    idx, idx2 = unstriped(offs), unstriped(offs2)
    xq = unpack_weight(x_words, x_scales, "e4m3")[:, idx]
    a = by_expert(wg, xq, G, C1)
    y = by_expert(we, mxq(a[:, idx2], 0, "e4m3"), E, C2)
    out = np.zeros((N, T))
    out[:, unstriped(dst)] = f64(gate[:1]) * y
    out_0 = out
    return (out_0,) + planes(out_0)

@@ -1,0 +1,280 @@
+from contextlib import ExitStack
+
+import concourse.mybir as mybir
+from concourse.masks import make_identity
+
+K, T, G, C1, E, C2, H, N = 1024, 768, 3, 256, 6, 128, 512, 512
+FLOPS = 2 * T * (K * H + H * N)
+
+F32 = mybir.dt.float32
+BF16 = mybir.dt.bfloat16
+I32 = mybir.dt.int32
+U32 = mybir.dt.uint32
+U16 = mybir.dt.uint16
+U8 = mybir.dt.uint8
+FP8X4 = mybir.dt.float8_e4m3fn_x4
+FP4X4 = mybir.dt.float4_e2m1fn_x4
+COPY = mybir.ActivationFunctionType.Copy
+MULT = mybir.AluOpType.mult
+
+P = 128
+PASSES = K // 512
+LIST = 16
+ON_VECTOR = [(2, 1), (2, 2), (2, 3)]
+
+
+def tile_moe_hie_none_kernel(
+    tc, x_words, x_scales, wg_words, wg_scales, we_words, we_scales, gate, offs, offs2, dst, out_0, out_1, out_2
+):
+    nc = tc.nc
+    with ExitStack() as ctx:
+        keep = ctx.enter_context(tc.tile_pool(name="keep", bufs=1))
+        psum = ctx.enter_context(tc.psum_pool(name="psum", bufs=1))
+
+        def held(shape, dtype, name, tag=None):
+            return keep.tile(shape, dtype, name=name, tag=tag or name, align_bytes=64)
+
+        offs_sb = held([P, T // LIST], U16, "offs_sb")
+        offs2_sb = held([P, T // LIST], U16, "offs2_sb")
+        dst_sb = held([P, T // LIST], U16, "dst_sb")
+        xw = held([P, PASSES * T], U32, "xw")
+        xs = held([P, T], U8, "xs")
+        wgw = [held([P, PASSES * H], U32, "wgw%d" % f) for f in range(G)]
+        wgs = held([P, G * PASSES * H], U8, "wgs")
+        wew = [held([P, 2 * 2 * N], U8, "wew0"), held([P, 4 * 2 * N], U8, "wew1")]
+        wes = held([P, E * N], U8, "wes")
+        gate_sb = [held([P, C1], F32, "gate0"), held([P, 2 * C1], F32, "gate1")]
+        ident = held([P, P], F32, "ident")
+        win = [held([P, max(768, C1 * (f + 2))], F32, "win%d" % f) for f in range(G)]
+
+        nc.gpsimd.memset(xs[:].bitcast(I32), 0)
+        nc.vector.memset(wgs[:].bitcast(I32), 0)
+        nc.vector.memset(win[0][:, 512:768], 0.0)
+        nc.vector.memset(wes[:].bitcast(I32), 0)
+        nc.scalar.activation(win[1][:, 0:256], win[0][:, 512:768], COPY)
+        nc.scalar.activation(win[2][:, 0:256], win[0][:, 512:768], COPY)
+        nc.scalar.activation(win[2][:, 256:512], win[0][:, 512:768], COPY)
+        make_identity(nc, ident[:])
+
+        wg_rows = wg_scales.rearrange("f s b i -> b (f s) i").bitcast(I32)
+        we_rows = we_scales.rearrange("e s b n -> (s b) e n").bitcast(I32)
+
+        def load_group_words(f):
+            nc.sync.dma_start(
+                wgw[f][:].bitcast(I32).rearrange("p (s i) -> p s i", s=PASSES),
+                wg_words[f].rearrange("s p i d -> p s (i d)").bitcast(I32),
+            )
+
+        def load_expert_words(j, first, count):
+            nc.sync.dma_start(
+                wew[j][:].bitcast(I32).rearrange("p (e c) -> p e c", e=count),
+                we_words[first : first + count].rearrange("e s p c -> p (e s) c").bitcast(I32),
+            )
+
+        def load_scale_rows(plane, rows):
+            for q in range(4):
+                nc.sync.dma_start(
+                    plane[32 * q : 32 * q + 4, :].bitcast(I32).rearrange("p (e c) -> p e c", e=6),
+                    rows[4 * q : 4 * q + 4],
+                )
+
+        nc.sync.dma_start(offs_sb[:], offs)
+        nc.sync.dma_start(offs2_sb[:], offs2)
+        nc.sync.dma_start(dst_sb[:], dst)
+        for q in range(4):
+            nc.sync.dma_start(xs[32 * q : 32 * q + 8, :].bitcast(I32), x_scales[:, 4 * q : 4 * q + 4, :].bitcast(I32))
+        nc.sync.dma_start(
+            xw[:].bitcast(I32).rearrange("p (s t) -> p s t", s=PASSES),
+            x_words.rearrange("s p t d -> p s (t d)").bitcast(I32),
+        )
+        load_group_words(0)
+        load_scale_rows(wgs, wg_rows)
+        load_expert_words(0, 0, 2)
+        load_group_words(1)
+        load_group_words(2)
+        load_scale_rows(wes, we_rows)
+        load_expert_words(1, 2, 4)
+        nc.sync.dma_start(gate_sb[0][:], gate[:, 0:C1])
+        nc.sync.dma_start(gate_sb[1][:], gate[:, C1:T])
+
+        xg = [held([P, T], U32, "xg%d" % s) for s in range(PASSES)]
+        xgs = held([P, T], U8, "xgs")
+        wep = [held([P, 2 * N], U8, "wep%d" % e) for e in range(E)]
+        wesp = {}
+        banks = {}
+        codes = [held([P, C1], U32, "codes%d" % f) for f in range(G)]
+        cscal = [held([P, C1], U8, "cscal%d" % f) for f in range(G)]
+        ysb = {}
+
+        def entries(lst, lo, n):
+            return lst[:, lo // LIST : (lo + n) // LIST]
+
+        def gather_scales(lo, n):
+            nc.vector.tensor_copy(xgs[:, lo : lo + n], xs[:].indirect(entries(offs_sb, lo, n)))
+
+        def gather_tokens(lo, n):
+            cols = slice(lo, lo + n)
+            for s in range(PASSES):
+                nc.vector.tensor_copy(xg[s][:, cols], xw[:, s * T : (s + 1) * T].indirect(entries(offs_sb, lo, n)))
+
+        def first_layer(f, h):
+            cols = slice(f * C1 + h * P, f * C1 + (h + 1) * P)
+            acc = psum.tile([P, H], F32, name="acc", tag="acc%d" % h)
+            for s in range(PASSES):
+                lo = (PASSES * f + s) * H
+                nc.tensor.matmul_mx(
+                    out=acc[:],
+                    lhsT=xg[s][:, cols].bitcast(FP8X4),
+                    lhsT_scale=xgs[4 * s : P, cols],
+                    rhs=wgw[f][:, s * H : (s + 1) * H].bitcast(FP8X4),
+                    rhs_scale=wgs[:, lo : lo + H],
+                    start=(s == 0),
+                    stop=(s == PASSES - 1),
+                )
+            pairs = held([P, H], BF16, "pairs%d_%d" % (f, h))
+            nc.scalar.copy(
+                pairs[:].rearrange("s (u p e) -> s u p e", u=2, e=2),
+                acc[:].rearrange("s (p u e) -> s u p e", u=2, e=2),
+            )
+            turned = psum.tile([P, 2 * P], F32, name="turned", tag="turned%d" % h)
+            words = pairs[:].bitcast(F32)
+            for u in range(2):
+                nc.tensor.transpose(turned[:, u * P : (u + 1) * P], words[:, u * P : (u + 1) * P], ident[:])
+            place = win[f][:, f * C1 : (f + 2) * C1].rearrange("p (u c) -> p u c", u=2)
+            nc.scalar.copy(place[:, :, h * P : (h + 1) * P], turned[:].rearrange("p (u c) -> p u c", u=2))
+
+        def deal_expert_words(e):
+            j, place = (0, e) if e < 2 else (1, e - 2)
+            src = wew[j][:, place * 2 * N : (place + 1) * 2 * N].bitcast(U16)
+            nc.scalar.copy(
+                wep[e][:].bitcast(U16).rearrange("p (t m) -> p t m", t=4),
+                src.rearrange("p (m t) -> p t m", t=4),
+            )
+
+        def deal_expert_scales(f):
+            wesp[f] = keep.tile([P, 2 * N], U8, name="wesp%d" % f, tag="turn%d" % (f - 1), align_bytes=64)
+            nc.vector.tensor_copy(
+                wesp[f][:].rearrange("p (e t m) -> p e t m", e=2, t=4),
+                wes[:, 2 * f * N : (2 * f + 2) * N].rearrange("p (e m t) -> p e t m", e=2, t=4),
+            )
+
+        def regroup(f):
+            width = max(512, C1 * (f + 1))
+            picked = keep.tile([P, 2 * C1], U32, name="picked%d" % f, tag="turn%d" % f if f < 2 else "gate0", align_bytes=64)
+            for u in range(2):
+                window = win[f][:, u * C1 : u * C1 + width].bitcast(U32)
+                nc.vector.tensor_copy(
+                    picked[:, u * C1 : (u + 1) * C1], window.indirect(entries(offs2_sb, f * C1, C1))
+                )
+            woven = held([P, 4 * C1], BF16, "woven%d" % f, "gate0" if f == 1 else None)
+            nc.vector.tensor_copy(
+                woven[:].bitcast(I32).rearrange("p (c u) -> p c u", u=2),
+                picked[:].bitcast(I32).rearrange("p (u c) -> p c u", u=2),
+            )
+            return woven
+
+        def quantize(f, woven):
+            nc.vector.quantize_mx(out=codes[f][:].bitcast(FP8X4), scales=cscal[f][:], in_=woven[:])
+
+        def second_layer(f):
+            for j in range(2):
+                tag = ["acc1", "turned1"][j] if f == 0 else "bank%d_%d" % (f, j)
+                bank = psum.tile([P, 2 * C1], F32, name="bank", tag=tag)
+                for t in (2 * j, 2 * j + 1):
+                    for h in range(2):
+                        e = 2 * f + h
+                        lo = (t % 2) * C1 + h * P
+                        nc.tensor.matmul_mx(
+                            out=bank[:, lo : lo + P],
+                            lhsT=wep[e][:, t * 2 * P : (t + 1) * 2 * P].bitcast(FP4X4),
+                            lhsT_scale=wesp[f][:, h * N + t * P : h * N + (t + 1) * P],
+                            rhs=codes[f][:, h * P : (h + 1) * P].bitcast(FP8X4),
+                            rhs_scale=cscal[f][:, h * P : (h + 1) * P],
+                            start=True,
+                            stop=True,
+                        )
+                banks[f, j] = bank
+
+        def weigh(f, j, weighed):
+            weights = gate_sb[0][:] if f == 0 else gate_sb[1][:, (f - 1) * C1 : f * C1]
+            nc.vector.tensor_tensor(
+                weighed.rearrange("p (t c) -> p t c", t=2),
+                banks[f, j][:].rearrange("p (t c) -> p t c", t=2),
+                weights.unsqueeze(1).to_broadcast([P, 2, C1]),
+                MULT,
+            )
+            for t in range(2):
+                ysb[f, 2 * j + t] = weighed[:, t * C1 : (t + 1) * C1]
+
+        def scatter(f, t):
+            window = res[t][:].indirect(entries(dst_sb, f * C1, C1))
+            if (f, t) in ON_VECTOR:
+                nc.vector.tensor_copy(window, ysb[f, t])
+            else:
+                nc.scalar.activation(window, ysb[f, t], COPY)
+
+        gather_scales(0, T // 2)
+        gather_tokens(0, P)
+        first_layer(0, 0)
+        gather_tokens(P, P)
+        first_layer(0, 1)
+        gather_scales(T // 2, T // 2)
+        for f in (1, 2):
+            gather_tokens(f * C1, C1)
+            first_layer(f, 0)
+            first_layer(f, 1)
+        for e in range(E):
+            deal_expert_words(e)
+        deal_expert_scales(0)
+        woven = regroup(0)
+        deal_expert_scales(1)
+        quantize(0, woven)
+        second_layer(0)
+        y0 = held([P, 4 * C1], F32, "y0")
+        weigh(0, 0, y0[:, 0 : 2 * C1])
+        weigh(0, 1, y0[:, 2 * C1 : 4 * C1])
+        woven = regroup(1)
+        deal_expert_scales(2)
+        quantize(1, woven)
+        second_layer(1)
+        weigh(1, 0, held([P, 2 * C1], F32, "y1_0")[:])
+        woven = regroup(2)
+        quantize(2, woven)
+        second_layer(2)
+        weigh(1, 1, held([P, 2 * C1], F32, "y1_1", "woven2")[:])
+        weigh(2, 0, held([P, 2 * C1], F32, "y2_0")[:])
+        weigh(2, 1, held([P, 2 * C1], F32, "y2_1")[:])
+        res = [held([P, T], F32, "res%d" % t) for t in range(4)]
+        for f, t in [(0, 0), (0, 1), (0, 2), (0, 3), (1, 0)] + ON_VECTOR + [(2, 0), (1, 1), (1, 2), (1, 3)]:
+            scatter(f, t)
+
+        rows = out_0.rearrange("(p t) c -> t p c", t=4)
+        fin = held([P, 4 * T], BF16, "fin")
+        fin4 = fin[:].rearrange("p (c t) -> p c t", t=4)
+        ocodes = held([P, T], U32, "ocodes")
+        oscal = held([P, T], U8, "oscal")
+        for t in range(4):
+            nc.sync.dma_start(rows[t], res[t][:])
+        for t in range(3):
+            nc.vector.tensor_copy(fin4[:, :, t], res[t][:])
+        words_out = out_1[0].rearrange("p c d -> p (c d)").bitcast(I32)
+
+        def last_plane(j):
+            cols = slice(j * C1, (j + 1) * C1)
+            nc.vector.tensor_copy(fin4[:, cols, 3], res[3][:, cols])
+
+        def hand_on(j):
+            cols = slice(j * C1, (j + 1) * C1)
+            nc.vector.quantize_mx(
+                out=ocodes[:, cols].bitcast(FP8X4), scales=oscal[:, cols], in_=fin[:, 4 * j * C1 : 4 * (j + 1) * C1]
+            )
+            nc.sync.dma_start(words_out[:, cols], ocodes[:, cols].bitcast(I32))
+
+        last_plane(0)
+        last_plane(1)
+        hand_on(0)
+        last_plane(2)
+        hand_on(1)
+        hand_on(2)
+        for q in range(4):
+            nc.scalar.dma_start(out_2[0, 4 * q : 4 * q + 4, :].bitcast(I32), oscal[32 * q : 32 * q + 4, :].bitcast(I32))

@@ -20,7 +20,6 @@ MULT = mybir.AluOpType.mult
 P = 128
 PASSES = K // 512
 LIST = 16
-ON_VECTOR = [(2, 1), (2, 2), (2, 3)]
 
 
 def tile_moe_hie_none_kernel(
@@ -91,17 +90,16 @@ def tile_moe_hie_none_kernel(
         load_scale_rows(wgs, wg_rows)
         load_expert_words(0, 0, 2)
         load_group_words(1)
+        load_expert_words(1, 2, 4)
         load_group_words(2)
         load_scale_rows(wes, we_rows)
-        load_expert_words(1, 2, 4)
         nc.sync.dma_start(gate_sb[0][:], gate[:, 0:C1])
         nc.sync.dma_start(gate_sb[1][:], gate[:, C1:T])
 
         xg = [held([P, T], U32, "xg%d" % s) for s in range(PASSES)]
         xgs = held([P, T], U8, "xgs")
-        wep = [held([P, 2 * N], U8, "wep%d" % e) for e in range(E)]
+        wep = {}
         wesp = {}
-        banks = {}
         codes = [held([P, C1], U32, "codes%d" % f) for f in range(G)]
         cscal = [held([P, C1], U8, "cscal%d" % f) for f in range(G)]
         ysb = {}
@@ -119,7 +117,7 @@ def tile_moe_hie_none_kernel(
 
         def first_layer(f, h):
             cols = slice(f * C1 + h * P, f * C1 + (h + 1) * P)
-            acc = psum.tile([P, H], F32, name="acc", tag="acc%d" % h)
+            acc = psum.tile([P, H], F32, name="acc", tag="acc%d" % ((2 * f + h) % 3))
             for s in range(PASSES):
                 lo = (PASSES * f + s) * H
                 nc.tensor.matmul_mx(
@@ -131,7 +129,7 @@ def tile_moe_hie_none_kernel(
                     start=(s == 0),
                     stop=(s == PASSES - 1),
                 )
-            pairs = held([P, H], BF16, "pairs%d_%d" % (f, h))
+            pairs = held([P, H], BF16, "pairs%d_%d" % (f, h), "wew0" if f + h == 0 else None)
             nc.scalar.copy(
                 pairs[:].rearrange("s (u p e) -> s u p e", u=2, e=2),
                 acc[:].rearrange("s (p u e) -> s u p e", u=2, e=2),
@@ -143,7 +141,8 @@ def tile_moe_hie_none_kernel(
             place = win[f][:, f * C1 : (f + 2) * C1].rearrange("p (u c) -> p u c", u=2)
             nc.scalar.copy(place[:, :, h * P : (h + 1) * P], turned[:].rearrange("p (u c) -> p u c", u=2))
 
-        def deal_expert_words(e):
+        def deal_expert_words(e, tag=None):
+            wep[e] = held([P, 2 * N], U8, "wep%d" % e, tag)
             j, place = (0, e) if e < 2 else (1, e - 2)
             src = wew[j][:, place * 2 * N : (place + 1) * 2 * N].bitcast(U16)
             nc.scalar.copy(
@@ -151,68 +150,72 @@ def tile_moe_hie_none_kernel(
                 src.rearrange("p (m t) -> p t m", t=4),
             )
 
-        def deal_expert_scales(f):
-            wesp[f] = keep.tile([P, 2 * N], U8, name="wesp%d" % f, tag="turn%d" % (f - 1), align_bytes=64)
+        def deal_expert_scales(f, tag):
+            wesp[f] = held([P, 2 * N], U8, "wesp%d" % f, tag)
             nc.vector.tensor_copy(
                 wesp[f][:].rearrange("p (e t m) -> p e t m", e=2, t=4),
                 wes[:, 2 * f * N : (2 * f + 2) * N].rearrange("p (e m t) -> p e t m", e=2, t=4),
             )
 
-        def regroup(f):
+        def regroup(f, lo, n, picked_tag=None, woven_tag=None):
             width = max(512, C1 * (f + 1))
-            picked = keep.tile([P, 2 * C1], U32, name="picked%d" % f, tag="turn%d" % f if f < 2 else "gate0", align_bytes=64)
+            picked = held([P, 2 * n], U32, "picked%d_%d" % (f, lo), picked_tag)
             for u in range(2):
                 window = win[f][:, u * C1 : u * C1 + width].bitcast(U32)
                 nc.vector.tensor_copy(
-                    picked[:, u * C1 : (u + 1) * C1], window.indirect(entries(offs2_sb, f * C1, C1))
+                    picked[:, u * n : (u + 1) * n], window.indirect(entries(offs2_sb, f * C1 + lo, n))
                 )
-            woven = held([P, 4 * C1], BF16, "woven%d" % f, "gate0" if f == 1 else None)
+            woven = held([P, 4 * n], BF16, "woven%d_%d" % (f, lo), woven_tag)
             nc.vector.tensor_copy(
                 woven[:].bitcast(I32).rearrange("p (c u) -> p c u", u=2),
                 picked[:].bitcast(I32).rearrange("p (u c) -> p c u", u=2),
             )
             return woven
 
-        def quantize(f, woven):
-            nc.vector.quantize_mx(out=codes[f][:].bitcast(FP8X4), scales=cscal[f][:], in_=woven[:])
+        def quantize(f, lo, n, woven):
+            cols = slice(lo, lo + n)
+            nc.vector.quantize_mx(out=codes[f][:, cols].bitcast(FP8X4), scales=cscal[f][:, cols], in_=woven[:])
 
-        def second_layer(f):
-            for j in range(2):
-                tag = ["acc1", "turned1"][j] if f == 0 else "bank%d_%d" % (f, j)
-                bank = psum.tile([P, 2 * C1], F32, name="bank", tag=tag)
-                for t in (2 * j, 2 * j + 1):
-                    for h in range(2):
-                        e = 2 * f + h
-                        lo = (t % 2) * C1 + h * P
-                        nc.tensor.matmul_mx(
-                            out=bank[:, lo : lo + P],
-                            lhsT=wep[e][:, t * 2 * P : (t + 1) * 2 * P].bitcast(FP4X4),
-                            lhsT_scale=wesp[f][:, h * N + t * P : h * N + (t + 1) * P],
-                            rhs=codes[f][:, h * P : (h + 1) * P].bitcast(FP8X4),
-                            rhs_scale=cscal[f][:, h * P : (h + 1) * P],
-                            start=True,
-                            stop=True,
-                        )
-                banks[f, j] = bank
+        def second_layer(f, planes, experts, tag):
+            bank = psum.tile([P, len(planes), len(experts), C2], F32, name="bank", tag=tag)
+            for j, t in enumerate(planes):
+                for k, h in enumerate(experts):
+                    nc.tensor.matmul_mx(
+                        out=bank[:, j, k, :],
+                        lhsT=wep[2 * f + h][:, t * 2 * P : (t + 1) * 2 * P].bitcast(FP4X4),
+                        lhsT_scale=wesp[f][:, h * N + t * P : h * N + (t + 1) * P],
+                        rhs=codes[f][:, h * P : (h + 1) * P].bitcast(FP8X4),
+                        rhs_scale=cscal[f][:, h * P : (h + 1) * P],
+                        start=True,
+                        stop=True,
+                    )
+            return bank
 
-        def weigh(f, j, weighed):
-            weights = gate_sb[0][:] if f == 0 else gate_sb[1][:, (f - 1) * C1 : f * C1]
+        def weigh(f, planes, experts, bank, tag=None):
+            lo, n = experts[0] * C2, len(experts) * C2
+            weighed = held([P, len(planes) * n], F32, "ysb%d_%d_%d" % (f, planes[0], experts[0]), tag)
+            first = lo if f == 0 else (f - 1) * C1 + lo
+            weights = gate_sb[min(f, 1)][:, first : first + n]
             nc.vector.tensor_tensor(
-                weighed.rearrange("p (t c) -> p t c", t=2),
-                banks[f, j][:].rearrange("p (t c) -> p t c", t=2),
-                weights.unsqueeze(1).to_broadcast([P, 2, C1]),
+                weighed[:].rearrange("p (t c) -> p t c", c=n),
+                bank[:].rearrange("p t k c -> p t (k c)"),
+                weights.unsqueeze(1).to_broadcast([P, len(planes), n]),
                 MULT,
             )
-            for t in range(2):
-                ysb[f, 2 * j + t] = weighed[:, t * C1 : (t + 1) * C1]
+            for j, t in enumerate(planes):
+                for k, h in enumerate(experts):
+                    ysb[f, t, h] = (weighed, j * n + k * C2)
 
-        def scatter(f, t):
-            window = res[t][:].indirect(entries(dst_sb, f * C1, C1))
-            if (f, t) in ON_VECTOR:
-                nc.vector.tensor_copy(window, ysb[f, t])
+        def scatter(on_vector, f, t, h=0, n=C1):
+            weighed, lo = ysb[f, t, h]
+            window = res[t][:].indirect(entries(dst_sb, f * C1 + h * C2, n))
+            if on_vector:
+                nc.vector.tensor_copy(window, weighed[:, lo : lo + n])
             else:
-                nc.scalar.activation(window, ysb[f, t], COPY)
+                nc.scalar.activation(window, weighed[:, lo : lo + n], COPY)
 
+        deal_expert_words(0)
+        deal_expert_words(1)
         gather_scales(0, T // 2)
         gather_tokens(0, P)
         first_layer(0, 0)
@@ -223,45 +226,64 @@ def tile_moe_hie_none_kernel(
             gather_tokens(f * C1, C1)
             first_layer(f, 0)
             first_layer(f, 1)
-        for e in range(E):
-            deal_expert_words(e)
-        deal_expert_scales(0)
-        woven = regroup(0)
-        deal_expert_scales(1)
-        quantize(0, woven)
-        second_layer(0)
-        y0 = held([P, 4 * C1], F32, "y0")
-        weigh(0, 0, y0[:, 0 : 2 * C1])
-        weigh(0, 1, y0[:, 2 * C1 : 4 * C1])
-        woven = regroup(1)
-        deal_expert_scales(2)
-        quantize(1, woven)
-        second_layer(1)
-        weigh(1, 0, held([P, 2 * C1], F32, "y1_0")[:])
-        woven = regroup(2)
-        quantize(2, woven)
-        second_layer(2)
-        weigh(1, 1, held([P, 2 * C1], F32, "y1_1", "woven2")[:])
-        weigh(2, 0, held([P, 2 * C1], F32, "y2_0")[:])
-        weigh(2, 1, held([P, 2 * C1], F32, "y2_1")[:])
+        for e, tag in zip(range(2, E), ["pairs1_1", "pairs2_0", "xg0", "pairs2_1"]):
+            deal_expert_words(e, tag)
+        deal_expert_scales(0, None)
+        quantize(0, 0, C2, regroup(0, 0, C2))
+        bank_a = second_layer(0, (0, 1, 2, 3), (0,), "bank0")
+        woven = regroup(0, C2, C2)
+        deal_expert_scales(1, "picked0_128")
+        quantize(0, C2, C2, woven)
+        bank_b = second_layer(0, (0, 1, 2, 3), (1,), "bank1")
+        weigh(0, (0, 1, 2, 3), (0,), bank_a)
+        weigh(0, (0, 1, 2, 3), (1,), bank_b)
+        woven = regroup(1, 0, C1, None, "gate0")
+        deal_expert_scales(2, "picked1_0")
+        quantize(1, 0, C1, woven)
+        bank_a = second_layer(1, (0, 1), (0, 1), "bank2")
+        bank_b = second_layer(1, (2, 3), (0, 1), "acc0")
+        weigh(1, (0, 1), (0, 1), bank_a)
+        quantize(2, 0, C1, regroup(2, 0, C1, "gate0"))
+        bank_c = second_layer(2, (0, 1), (0, 1), "bank0")
+        bank_d = second_layer(2, (2, 3), (0, 1), "bank1")
+        weigh(1, (2, 3), (0, 1), bank_b, "woven2_0")
+        weigh(2, (0, 1), (0, 1), bank_c)
+        weigh(2, (2, 3), (0, 1), bank_d)
         res = [held([P, T], F32, "res%d" % t) for t in range(4)]
-        for f, t in [(0, 0), (0, 1), (0, 2), (0, 3), (1, 0)] + ON_VECTOR + [(2, 0), (1, 1), (1, 2), (1, 3)]:
-            scatter(f, t)
+        for h in range(2):
+            for t in range(4):
+                scatter(False, 0, t, h, C2)
+        scatter(False, 1, 0)
+        scatter(False, 1, 1)
+        scatter(True, 2, 0)
+        scatter(True, 2, 1)
+        scatter(False, 1, 2, 0, C2)
+        scatter(True, 1, 2, 1, C2)
+        scatter(True, 2, 2)
+        scatter(False, 1, 3)
+        scatter(False, 2, 3)
 
         rows = out_0.rearrange("(p t) c -> t p c", t=4)
+        stage = held([P, 4 * T], F32, "stage")
         fin = held([P, 4 * T], BF16, "fin")
-        fin4 = fin[:].rearrange("p (c t) -> p c t", t=4)
         ocodes = held([P, T], U32, "ocodes")
         oscal = held([P, T], U8, "oscal")
-        for t in range(4):
+        for t in range(2):
+            nc.sync.dma_start(stage[:, t * T : (t + 1) * T], res[t][:])
             nc.sync.dma_start(rows[t], res[t][:])
-        for t in range(3):
-            nc.vector.tensor_copy(fin4[:, :, t], res[t][:])
+        nc.vector.tensor_copy(stage[:, 2 * T : 3 * T], res[2][:])
+        nc.vector.tensor_copy(stage[:, 3 * T : 3 * T + C1], res[3][:, 0:C1])
+        nc.scalar.copy(stage[:, 3 * T + C1 : 4 * T], res[3][:, C1:T])
+        for t in range(2, 4):
+            nc.sync.dma_start(rows[t], res[t][:])
         words_out = out_1[0].rearrange("p c d -> p (c d)").bitcast(I32)
 
-        def last_plane(j):
+        def weave_rows(j, copy):
             cols = slice(j * C1, (j + 1) * C1)
-            nc.vector.tensor_copy(fin4[:, cols, 3], res[3][:, cols])
+            copy(
+                fin[:].rearrange("p (c t) -> p c t", t=4)[:, cols, :],
+                stage[:].rearrange("p (t c) -> p c t", t=4)[:, cols, :],
+            )
 
         def hand_on(j):
             cols = slice(j * C1, (j + 1) * C1)
@@ -270,11 +292,10 @@ def tile_moe_hie_none_kernel(
             )
             nc.sync.dma_start(words_out[:, cols], ocodes[:, cols].bitcast(I32))
 
-        last_plane(0)
-        last_plane(1)
-        hand_on(0)
-        last_plane(2)
-        hand_on(1)
-        hand_on(2)
+        weave_rows(0, nc.vector.tensor_copy)
+        weave_rows(1, nc.vector.tensor_copy)
+        weave_rows(2, nc.scalar.copy)
+        for j in range(3):
+            hand_on(j)
         for q in range(4):
             nc.scalar.dma_start(out_2[0, 4 * q : 4 * q + 4, :].bitcast(I32), oscal[32 * q : 32 * q + 4, :].bitcast(I32))

@@ -39,7 +39,7 @@ def tile_moe_hie_none_kernel(
         xw = held([P, PASSES * T], U32, "xw")
         xs = held([P, T], U8, "xs")
         wgw = [held([P, PASSES * H], U32, "wgw%d" % f) for f in range(G)]
-        wgs = held([P, G * PASSES * H], U8, "wgs")
+        wgs = [held([P, H], U8, "wgs%d" % j) for j in range(2)]
         wew = [held([P, 2 * 2 * N], U8, "wew0"), held([P, 4 * 2 * N], U8, "wew1")]
         wes = held([P, E * N], U8, "wes")
         gate_sb = [held([P, C1], F32, "gate0"), held([P, 2 * C1], F32, "gate1")]
@@ -47,15 +47,16 @@ def tile_moe_hie_none_kernel(
         win = [held([P, max(768, C1 * (f + 2))], F32, "win%d" % f) for f in range(G)]
 
         nc.gpsimd.memset(xs[:].bitcast(I32), 0)
-        nc.vector.memset(wgs[:].bitcast(I32), 0)
+        nc.vector.memset(wgs[0][:].bitcast(I32), 0)
         nc.vector.memset(win[0][:, 512:768], 0.0)
         nc.vector.memset(wes[:].bitcast(I32), 0)
+        nc.vector.memset(wgs[1][:].bitcast(I32), 0)
         nc.scalar.activation(win[1][:, 0:256], win[0][:, 512:768], COPY)
         nc.scalar.activation(win[2][:, 0:256], win[0][:, 512:768], COPY)
         nc.scalar.activation(win[2][:, 256:512], win[0][:, 512:768], COPY)
         make_identity(nc, ident[:])
 
-        wg_rows = wg_scales.rearrange("f s b i -> b (f s) i").bitcast(I32)
+        wg_rows = wg_scales.rearrange("f s b i -> (f s) b i").bitcast(I32)
         we_rows = we_scales.rearrange("e s b n -> (s b) e n").bitcast(I32)
 
         def load_group_words(f):
@@ -70,11 +71,11 @@ def tile_moe_hie_none_kernel(
                 we_words[first : first + count].rearrange("e s p c -> p (e s) c").bitcast(I32),
             )
 
-        def load_scale_rows(plane, rows):
+        def load_group_scales(j, first, count):
             for q in range(4):
                 nc.sync.dma_start(
-                    plane[32 * q : 32 * q + 4, :].bitcast(I32).rearrange("p (e c) -> p e c", e=6),
-                    rows[4 * q : 4 * q + 4],
+                    wgs[j][32 * q : 32 * q + 4 * count, :].bitcast(I32),
+                    wg_rows[first : first + count, 4 * q : 4 * q + 4, :],
                 )
 
         nc.sync.dma_start(offs_sb[:], offs)
@@ -87,12 +88,17 @@ def tile_moe_hie_none_kernel(
             x_words.rearrange("s p t d -> p s (t d)").bitcast(I32),
         )
         load_group_words(0)
-        load_scale_rows(wgs, wg_rows)
+        load_group_scales(0, 0, 4)
         load_expert_words(0, 0, 2)
         load_group_words(1)
-        load_expert_words(1, 2, 4)
+        for q in range(4):
+            nc.sync.dma_start(
+                wes[32 * q : 32 * q + 4, :].bitcast(I32).rearrange("p (e c) -> p e c", e=E),
+                we_rows[4 * q : 4 * q + 4],
+            )
+        load_group_scales(1, 4, 2)
         load_group_words(2)
-        load_scale_rows(wes, we_rows)
+        load_expert_words(1, 2, 4)
         nc.sync.dma_start(gate_sb[0][:], gate[:, 0:C1])
         nc.sync.dma_start(gate_sb[1][:], gate[:, C1:T])
 
@@ -119,13 +125,13 @@ def tile_moe_hie_none_kernel(
             cols = slice(f * C1 + h * P, f * C1 + (h + 1) * P)
             acc = psum.tile([P, H], F32, name="acc", tag="acc%d" % ((2 * f + h) % 3))
             for s in range(PASSES):
-                lo = (PASSES * f + s) * H
+                row = 4 * ((PASSES * f + s) % 4)
                 nc.tensor.matmul_mx(
                     out=acc[:],
                     lhsT=xg[s][:, cols].bitcast(FP8X4),
                     lhsT_scale=xgs[4 * s : P, cols],
                     rhs=wgw[f][:, s * H : (s + 1) * H].bitcast(FP8X4),
-                    rhs_scale=wgs[:, lo : lo + H],
+                    rhs_scale=wgs[f // 2][row:P, :],
                     start=(s == 0),
                     stop=(s == PASSES - 1),
                 )
@@ -167,8 +173,8 @@ def tile_moe_hie_none_kernel(
                 )
             woven = held([P, 4 * n], BF16, "woven%d_%d" % (f, lo), woven_tag)
             nc.vector.tensor_copy(
-                woven[:].bitcast(I32).rearrange("p (c u) -> p c u", u=2),
-                picked[:].bitcast(I32).rearrange("p (u c) -> p c u", u=2),
+                woven[:].bitcast(I32).rearrange("p (c i u) -> p c u i", i=4, u=2),
+                picked[:].bitcast(I32).rearrange("p (u c i) -> p c u i", i=4, u=2),
             )
             return woven
 
@@ -254,14 +260,12 @@ def tile_moe_hie_none_kernel(
             for t in range(4):
                 scatter(False, 0, t, h, C2)
         scatter(False, 1, 0)
-        scatter(False, 1, 1)
-        scatter(True, 2, 0)
         scatter(True, 2, 1)
-        scatter(False, 1, 2, 0, C2)
-        scatter(True, 1, 2, 1, C2)
-        scatter(True, 2, 2)
-        scatter(False, 1, 3)
-        scatter(False, 2, 3)
+        scatter(True, 2, 0)
+        scatter(False, 1, 1)
+        for f in (1, 2):
+            scatter(True, f, 2)
+            scatter(False, f, 3)
 
         rows = out_0.rearrange("(p t) c -> t p c", t=4)
         stage = held([P, 4 * T], F32, "stage")
@@ -279,10 +283,10 @@ def tile_moe_hie_none_kernel(
         words_out = out_1[0].rearrange("p c d -> p (c d)").bitcast(I32)
 
         def weave_rows(j, copy):
-            cols = slice(j * C1, (j + 1) * C1)
+            fours = slice(j * C1 // 4, (j + 1) * C1 // 4)
             copy(
-                fin[:].rearrange("p (c t) -> p c t", t=4)[:, cols, :],
-                stage[:].rearrange("p (t c) -> p c t", t=4)[:, cols, :],
+                fin[:].rearrange("p (c i t) -> p c t i", i=4, t=4)[:, fours],
+                stage[:].rearrange("p (t c i) -> p c t i", i=4, t=4)[:, fours],
             )
 
         def hand_on(j):

@@ -91,13 +91,13 @@ def tile_moe_hie_none_kernel(
         load_group_scales(0, 0, 4)
         load_expert_words(0, 0, 2)
         load_group_words(1)
+        load_group_words(2)
+        load_group_scales(1, 4, 2)
         for q in range(4):
             nc.sync.dma_start(
                 wes[32 * q : 32 * q + 4, :].bitcast(I32).rearrange("p (e c) -> p e c", e=E),
                 we_rows[4 * q : 4 * q + 4],
             )
-        load_group_scales(1, 4, 2)
-        load_group_words(2)
         load_expert_words(1, 2, 4)
         nc.sync.dma_start(gate_sb[0][:], gate[:, 0:C1])
         nc.sync.dma_start(gate_sb[1][:], gate[:, C1:T])
@@ -236,7 +236,7 @@ def tile_moe_hie_none_kernel(
             deal_expert_words(e, tag)
         deal_expert_scales(0, None)
         quantize(0, 0, C2, regroup(0, 0, C2))
-        bank_a = second_layer(0, (0, 1, 2, 3), (0,), "bank0")
+        bank_a = second_layer(0, (0, 1, 2, 3), (0,), "acc2")
         woven = regroup(0, C2, C2)
         deal_expert_scales(1, "picked0_128")
         quantize(0, C2, C2, woven)
@@ -250,22 +250,19 @@ def tile_moe_hie_none_kernel(
         bank_b = second_layer(1, (2, 3), (0, 1), "acc0")
         weigh(1, (0, 1), (0, 1), bank_a)
         quantize(2, 0, C1, regroup(2, 0, C1, "gate0"))
-        bank_c = second_layer(2, (0, 1), (0, 1), "bank0")
-        bank_d = second_layer(2, (2, 3), (0, 1), "bank1")
+        bank_d = second_layer(2, (2, 3), (0, 1), "bank0")
+        bank_c = second_layer(2, (0, 1), (0, 1), "bank1")
         weigh(1, (2, 3), (0, 1), bank_b, "woven2_0")
-        weigh(2, (0, 1), (0, 1), bank_c)
         weigh(2, (2, 3), (0, 1), bank_d)
+        weigh(2, (0, 1), (0, 1), bank_c)
         res = [held([P, T], F32, "res%d" % t) for t in range(4)]
         for h in range(2):
             for t in range(4):
                 scatter(False, 0, t, h, C2)
-        scatter(False, 1, 0)
-        scatter(True, 2, 1)
-        scatter(True, 2, 0)
-        scatter(False, 1, 1)
-        for f in (1, 2):
-            scatter(True, f, 2)
-            scatter(False, f, 3)
+        for f, t in [(1, 0), (1, 1), (1, 3), (2, 3)]:
+            scatter(False, f, t)
+        for f, t in [(2, 2), (2, 0), (2, 1), (1, 2)]:
+            scatter(True, f, t)
 
         rows = out_0.rearrange("(p t) c -> t p c", t=4)
         stage = held([P, 4 * T], F32, "stage")
@@ -278,8 +275,8 @@ def tile_moe_hie_none_kernel(
         nc.vector.tensor_copy(stage[:, 2 * T : 3 * T], res[2][:])
         nc.vector.tensor_copy(stage[:, 3 * T : 3 * T + C1], res[3][:, 0:C1])
         nc.scalar.copy(stage[:, 3 * T + C1 : 4 * T], res[3][:, C1:T])
-        for t in range(2, 4):
-            nc.sync.dma_start(rows[t], res[t][:])
+        nc.sync.dma_start(rows[2], res[2][:])
+        nc.sync.dma_start(rows[3], stage[:, 3 * T : 4 * T])
         words_out = out_1[0].rearrange("p c d -> p (c d)").bitcast(I32)
 
         def weave_rows(j, copy):

@@ -19,7 +19,12 @@ MULT = mybir.AluOpType.mult
 
 P = 128
 PASSES = K // 512
+PLANES = 4
+QUADRANTS = 4
 LIST = 16
+E2M1_ROW = 2 * N
+ACC_BANKS = 3
+RUN = 4
 
 
 def tile_moe_hie_none_kernel(
@@ -40,20 +45,21 @@ def tile_moe_hie_none_kernel(
         xs = held([P, T], U8, "xs")
         wgw = [held([P, PASSES * H], U32, "wgw%d" % f) for f in range(G)]
         wgs = [held([P, H], U8, "wgs%d" % j) for j in range(2)]
-        wew = [held([P, 2 * 2 * N], U8, "wew0"), held([P, 4 * 2 * N], U8, "wew1")]
+        wew = [held([P, 2 * E2M1_ROW], U8, "wew0"), held([P, 4 * E2M1_ROW], U8, "wew1")]
         wes = held([P, E * N], U8, "wes")
         gate_sb = [held([P, C1], F32, "gate0"), held([P, 2 * C1], F32, "gate1")]
         ident = held([P, P], F32, "ident")
-        win = [held([P, max(768, C1 * (f + 2))], F32, "win%d" % f) for f in range(G)]
+        a_words = [held([P, C1 * max(3, f + 2)], F32, "a_words%d" % f) for f in range(G)]
 
         nc.gpsimd.memset(xs[:].bitcast(I32), 0)
         nc.vector.memset(wgs[0][:].bitcast(I32), 0)
-        nc.vector.memset(win[0][:, 512:768], 0.0)
+        zeros = a_words[0][:, 2 * C1 : 3 * C1]
+        nc.vector.memset(zeros, 0.0)
         nc.vector.memset(wes[:].bitcast(I32), 0)
         nc.vector.memset(wgs[1][:].bitcast(I32), 0)
-        nc.scalar.activation(win[1][:, 0:256], win[0][:, 512:768], COPY)
-        nc.scalar.activation(win[2][:, 0:256], win[0][:, 512:768], COPY)
-        nc.scalar.activation(win[2][:, 256:512], win[0][:, 512:768], COPY)
+        for f in range(1, G):
+            for j in range(f):
+                nc.scalar.activation(a_words[f][:, j * C1 : (j + 1) * C1], zeros, COPY)
         make_identity(nc, ident[:])
 
         wg_rows = wg_scales.rearrange("f s b i -> (f s) b i").bitcast(I32)
@@ -72,7 +78,7 @@ def tile_moe_hie_none_kernel(
             )
 
         def load_group_scales(j, first, count):
-            for q in range(4):
+            for q in range(QUADRANTS):
                 nc.sync.dma_start(
                     wgs[j][32 * q : 32 * q + 4 * count, :].bitcast(I32),
                     wg_rows[first : first + count, 4 * q : 4 * q + 4, :],
@@ -81,19 +87,21 @@ def tile_moe_hie_none_kernel(
         nc.sync.dma_start(offs_sb[:], offs)
         nc.sync.dma_start(offs2_sb[:], offs2)
         nc.sync.dma_start(dst_sb[:], dst)
-        for q in range(4):
-            nc.sync.dma_start(xs[32 * q : 32 * q + 8, :].bitcast(I32), x_scales[:, 4 * q : 4 * q + 4, :].bitcast(I32))
+        for q in range(QUADRANTS):
+            nc.sync.dma_start(
+                xs[32 * q : 32 * q + 4 * PASSES, :].bitcast(I32), x_scales[:, 4 * q : 4 * q + 4, :].bitcast(I32)
+            )
         nc.sync.dma_start(
             xw[:].bitcast(I32).rearrange("p (s t) -> p s t", s=PASSES),
             x_words.rearrange("s p t d -> p s (t d)").bitcast(I32),
         )
         load_group_words(0)
-        load_group_scales(0, 0, 4)
+        load_group_scales(0, 0, 2 * PASSES)
         load_expert_words(0, 0, 2)
         load_group_words(1)
         load_group_words(2)
-        load_group_scales(1, 4, 2)
-        for q in range(4):
+        load_group_scales(1, 2 * PASSES, PASSES)
+        for q in range(QUADRANTS):
             nc.sync.dma_start(
                 wes[32 * q : 32 * q + 4, :].bitcast(I32).rearrange("p (e c) -> p e c", e=E),
                 we_rows[4 * q : 4 * q + 4],
@@ -104,28 +112,29 @@ def tile_moe_hie_none_kernel(
 
         xg = [held([P, T], U32, "xg%d" % s) for s in range(PASSES)]
         xgs = held([P, T], U8, "xgs")
-        wep = {}
-        wesp = {}
+        dealt_words = {}
+        dealt_scales = {}
         codes = [held([P, C1], U32, "codes%d" % f) for f in range(G)]
-        cscal = [held([P, C1], U8, "cscal%d" % f) for f in range(G)]
-        ysb = {}
+        code_scales = [held([P, C1], U8, "code_scales%d" % f) for f in range(G)]
+        results = {}
 
-        def entries(lst, lo, n):
-            return lst[:, lo // LIST : (lo + n) // LIST]
+        def entries(list_sb, lo, n):
+            return list_sb[:, lo // LIST : (lo + n) // LIST]
 
         def gather_scales(lo, n):
             nc.vector.tensor_copy(xgs[:, lo : lo + n], xs[:].indirect(entries(offs_sb, lo, n)))
 
         def gather_tokens(lo, n):
-            cols = slice(lo, lo + n)
             for s in range(PASSES):
-                nc.vector.tensor_copy(xg[s][:, cols], xw[:, s * T : (s + 1) * T].indirect(entries(offs_sb, lo, n)))
+                window = xw[:, s * T : (s + 1) * T]
+                nc.vector.tensor_copy(xg[s][:, lo : lo + n], window.indirect(entries(offs_sb, lo, n)))
 
-        def first_layer(f, h):
-            cols = slice(f * C1 + h * P, f * C1 + (h + 1) * P)
-            acc = psum.tile([P, H], F32, name="acc", tag="acc%d" % ((2 * f + h) % 3))
+        def first_layer(f, h, pairs_tag=None):
+            block = 2 * f + h
+            cols = slice(block * P, (block + 1) * P)
+            acc = psum.tile([P, H], F32, name="acc", tag="acc%d" % (block % ACC_BANKS))
             for s in range(PASSES):
-                row = 4 * ((PASSES * f + s) % 4)
+                row = 4 * (PASSES * (f % 2) + s)
                 nc.tensor.matmul_mx(
                     out=acc[:],
                     lhsT=xg[s][:, cols].bitcast(FP8X4),
@@ -135,7 +144,7 @@ def tile_moe_hie_none_kernel(
                     start=(s == 0),
                     stop=(s == PASSES - 1),
                 )
-            pairs = held([P, H], BF16, "pairs%d_%d" % (f, h), "wew0" if f + h == 0 else None)
+            pairs = held([P, H], BF16, "pairs%d" % block, pairs_tag)
             nc.scalar.copy(
                 pairs[:].rearrange("s (u p e) -> s u p e", u=2, e=2),
                 acc[:].rearrange("s (p u e) -> s u p e", u=2, e=2),
@@ -144,54 +153,54 @@ def tile_moe_hie_none_kernel(
             words = pairs[:].bitcast(F32)
             for u in range(2):
                 nc.tensor.transpose(turned[:, u * P : (u + 1) * P], words[:, u * P : (u + 1) * P], ident[:])
-            place = win[f][:, f * C1 : (f + 2) * C1].rearrange("p (u c) -> p u c", u=2)
-            nc.scalar.copy(place[:, :, h * P : (h + 1) * P], turned[:].rearrange("p (u c) -> p u c", u=2))
+            halves = a_words[f][:, f * C1 : (f + 2) * C1].rearrange("p (u c) -> p u c", u=2)
+            nc.scalar.copy(halves[:, :, h * P : (h + 1) * P], turned[:].rearrange("p (u c) -> p u c", u=2))
 
         def deal_expert_words(e, tag=None):
-            wep[e] = held([P, 2 * N], U8, "wep%d" % e, tag)
+            dealt_words[e] = held([P, E2M1_ROW], U8, "dealt_words%d" % e, tag)
             j, place = (0, e) if e < 2 else (1, e - 2)
-            src = wew[j][:, place * 2 * N : (place + 1) * 2 * N].bitcast(U16)
+            src = wew[j][:, place * E2M1_ROW : (place + 1) * E2M1_ROW].bitcast(U16)
             nc.scalar.copy(
-                wep[e][:].bitcast(U16).rearrange("p (t m) -> p t m", t=4),
-                src.rearrange("p (m t) -> p t m", t=4),
+                dealt_words[e][:].bitcast(U16).rearrange("p (t m) -> p t m", t=PLANES),
+                src.rearrange("p (m t) -> p t m", t=PLANES),
             )
 
-        def deal_expert_scales(f, tag):
-            wesp[f] = held([P, 2 * N], U8, "wesp%d" % f, tag)
+        def deal_expert_scales(f, tag=None):
+            dealt_scales[f] = held([P, 2 * N], U8, "dealt_scales%d" % f, tag)
             nc.vector.tensor_copy(
-                wesp[f][:].rearrange("p (e t m) -> p e t m", e=2, t=4),
-                wes[:, 2 * f * N : (2 * f + 2) * N].rearrange("p (e m t) -> p e t m", e=2, t=4),
+                dealt_scales[f][:].rearrange("p (e t m) -> p e t m", e=2, t=PLANES),
+                wes[:, 2 * f * N : (2 * f + 2) * N].rearrange("p (e m t) -> p e t m", e=2, t=PLANES),
             )
 
         def regroup(f, lo, n, picked_tag=None, woven_tag=None):
-            width = max(512, C1 * (f + 1))
+            width = C1 * max(2, f + 1)
             picked = held([P, 2 * n], U32, "picked%d_%d" % (f, lo), picked_tag)
             for u in range(2):
-                window = win[f][:, u * C1 : u * C1 + width].bitcast(U32)
+                window = a_words[f][:, u * C1 : u * C1 + width].bitcast(U32)
                 nc.vector.tensor_copy(
                     picked[:, u * n : (u + 1) * n], window.indirect(entries(offs2_sb, f * C1 + lo, n))
                 )
             woven = held([P, 4 * n], BF16, "woven%d_%d" % (f, lo), woven_tag)
             nc.vector.tensor_copy(
-                woven[:].bitcast(I32).rearrange("p (c i u) -> p c u i", i=4, u=2),
-                picked[:].bitcast(I32).rearrange("p (u c i) -> p c u i", i=4, u=2),
+                woven[:].bitcast(I32).rearrange("p (c r u) -> p c u r", r=RUN, u=2),
+                picked[:].bitcast(I32).rearrange("p (u c r) -> p c u r", r=RUN, u=2),
             )
             return woven
 
         def quantize(f, lo, n, woven):
             cols = slice(lo, lo + n)
-            nc.vector.quantize_mx(out=codes[f][:, cols].bitcast(FP8X4), scales=cscal[f][:, cols], in_=woven[:])
+            nc.vector.quantize_mx(out=codes[f][:, cols].bitcast(FP8X4), scales=code_scales[f][:, cols], in_=woven[:])
 
         def second_layer(f, planes, experts, tag):
             bank = psum.tile([P, len(planes), len(experts), C2], F32, name="bank", tag=tag)
             for j, t in enumerate(planes):
-                for k, h in enumerate(experts):
+                for place, h in enumerate(experts):
                     nc.tensor.matmul_mx(
-                        out=bank[:, j, k, :],
-                        lhsT=wep[2 * f + h][:, t * 2 * P : (t + 1) * 2 * P].bitcast(FP4X4),
-                        lhsT_scale=wesp[f][:, h * N + t * P : h * N + (t + 1) * P],
-                        rhs=codes[f][:, h * P : (h + 1) * P].bitcast(FP8X4),
-                        rhs_scale=cscal[f][:, h * P : (h + 1) * P],
+                        out=bank[:, j, place, :],
+                        lhsT=dealt_words[2 * f + h][:, t * 2 * P : (t + 1) * 2 * P].bitcast(FP4X4),
+                        lhsT_scale=dealt_scales[f][:, h * N + t * P : h * N + (t + 1) * P],
+                        rhs=codes[f][:, h * C2 : (h + 1) * C2].bitcast(FP8X4),
+                        rhs_scale=code_scales[f][:, h * C2 : (h + 1) * C2],
                         start=True,
                         stop=True,
                     )
@@ -199,22 +208,22 @@ def tile_moe_hie_none_kernel(
 
         def weigh(f, planes, experts, bank, tag=None):
             lo, n = experts[0] * C2, len(experts) * C2
-            weighed = held([P, len(planes) * n], F32, "ysb%d_%d_%d" % (f, planes[0], experts[0]), tag)
+            weighed = held([P, len(planes) * n], F32, "weighed%d_%d_%d" % (f, planes[0], experts[0]), tag)
             first = lo if f == 0 else (f - 1) * C1 + lo
             weights = gate_sb[min(f, 1)][:, first : first + n]
             nc.vector.tensor_tensor(
                 weighed[:].rearrange("p (t c) -> p t c", c=n),
-                bank[:].rearrange("p t k c -> p t (k c)"),
+                bank[:].rearrange("p t h c -> p t (h c)"),
                 weights.unsqueeze(1).to_broadcast([P, len(planes), n]),
                 MULT,
             )
             for j, t in enumerate(planes):
-                for k, h in enumerate(experts):
-                    ysb[f, t, h] = (weighed, j * n + k * C2)
+                for place, h in enumerate(experts):
+                    results[f, t, h] = (weighed, j * n + place * C2)
 
         def scatter(on_vector, f, t, h=0, n=C1):
-            weighed, lo = ysb[f, t, h]
-            window = res[t][:].indirect(entries(dst_sb, f * C1 + h * C2, n))
+            weighed, lo = results[f, t, h]
+            window = plane_sb[t][:].indirect(entries(dst_sb, f * C1 + h * C2, n))
             if on_vector:
                 nc.vector.tensor_copy(window, weighed[:, lo : lo + n])
             else:
@@ -224,79 +233,79 @@ def tile_moe_hie_none_kernel(
         deal_expert_words(1)
         gather_scales(0, T // 2)
         gather_tokens(0, P)
-        first_layer(0, 0)
+        first_layer(0, 0, "wew0")
         gather_tokens(P, P)
         first_layer(0, 1)
         gather_scales(T // 2, T // 2)
-        for f in (1, 2):
+        for f in range(1, G):
             gather_tokens(f * C1, C1)
             first_layer(f, 0)
             first_layer(f, 1)
-        for e, tag in zip(range(2, E), ["pairs1_1", "pairs2_0", "xg0", "pairs2_1"]):
+        for e, tag in zip(range(2, E), ["pairs3", "pairs4", "xg0", "pairs5"]):
             deal_expert_words(e, tag)
-        deal_expert_scales(0, None)
+
+        every_plane, low_planes, high_planes, both = (0, 1, 2, 3), (0, 1), (2, 3), (0, 1)
+        deal_expert_scales(0)
         quantize(0, 0, C2, regroup(0, 0, C2))
-        bank_a = second_layer(0, (0, 1, 2, 3), (0,), "acc2")
+        sums_e0 = second_layer(0, every_plane, (0,), "acc%d" % ((2 * G - 1) % ACC_BANKS))
         woven = regroup(0, C2, C2)
-        deal_expert_scales(1, "picked0_128")
+        deal_expert_scales(1, "picked0_%d" % C2)
         quantize(0, C2, C2, woven)
-        bank_b = second_layer(0, (0, 1, 2, 3), (1,), "bank1")
-        weigh(0, (0, 1, 2, 3), (0,), bank_a)
-        weigh(0, (0, 1, 2, 3), (1,), bank_b)
+        sums_e1 = second_layer(0, every_plane, (1,), "bank1")
+        weigh(0, every_plane, (0,), sums_e0)
+        weigh(0, every_plane, (1,), sums_e1)
         woven = regroup(1, 0, C1, None, "gate0")
         deal_expert_scales(2, "picked1_0")
         quantize(1, 0, C1, woven)
-        bank_a = second_layer(1, (0, 1), (0, 1), "bank2")
-        bank_b = second_layer(1, (2, 3), (0, 1), "acc0")
-        weigh(1, (0, 1), (0, 1), bank_a)
+        low_1 = second_layer(1, low_planes, both, "bank2")
+        high_1 = second_layer(1, high_planes, both, "acc0")
+        weigh(1, low_planes, both, low_1)
         quantize(2, 0, C1, regroup(2, 0, C1, "gate0"))
-        bank_d = second_layer(2, (2, 3), (0, 1), "bank0")
-        bank_c = second_layer(2, (0, 1), (0, 1), "bank1")
-        weigh(1, (2, 3), (0, 1), bank_b, "woven2_0")
-        weigh(2, (2, 3), (0, 1), bank_d)
-        weigh(2, (0, 1), (0, 1), bank_c)
-        res = [held([P, T], F32, "res%d" % t) for t in range(4)]
+        high_2 = second_layer(2, high_planes, both, "bank0")
+        low_2 = second_layer(2, low_planes, both, "bank1")
+        weigh(1, high_planes, both, high_1, "woven2_0")
+        weigh(2, high_planes, both, high_2)
+        weigh(2, low_planes, both, low_2)
+
+        plane_sb = [held([P, T], F32, "plane_sb%d" % t) for t in range(PLANES)]
         for h in range(2):
-            for t in range(4):
+            for t in range(PLANES):
                 scatter(False, 0, t, h, C2)
         for f, t in [(1, 0), (1, 1), (1, 3), (2, 3)]:
             scatter(False, f, t)
         for f, t in [(2, 2), (2, 0), (2, 1), (1, 2)]:
             scatter(True, f, t)
 
-        rows = out_0.rearrange("(p t) c -> t p c", t=4)
-        stage = held([P, 4 * T], F32, "stage")
-        fin = held([P, 4 * T], BF16, "fin")
-        ocodes = held([P, T], U32, "ocodes")
-        oscal = held([P, T], U8, "oscal")
-        for t in range(2):
-            nc.sync.dma_start(stage[:, t * T : (t + 1) * T], res[t][:])
-            nc.sync.dma_start(rows[t], res[t][:])
-        nc.vector.tensor_copy(stage[:, 2 * T : 3 * T], res[2][:])
-        nc.vector.tensor_copy(stage[:, 3 * T : 3 * T + C1], res[3][:, 0:C1])
-        nc.scalar.copy(stage[:, 3 * T + C1 : 4 * T], res[3][:, C1:T])
-        nc.sync.dma_start(rows[2], res[2][:])
-        nc.sync.dma_start(rows[3], stage[:, 3 * T : 4 * T])
-        words_out = out_1[0].rearrange("p c d -> p (c d)").bitcast(I32)
+        rows = out_0.rearrange("(p t) c -> t p c", t=PLANES)
+        stage = held([P, PLANES * T], F32, "stage")
+        rounded = held([P, PLANES * T], BF16, "rounded")
+        out_codes = held([P, T], U32, "out_codes")
+        out_scales = held([P, T], U8, "out_scales")
+        for t in low_planes:
+            nc.sync.dma_start(stage[:, t * T : (t + 1) * T], plane_sb[t][:])
+            nc.sync.dma_start(rows[t], plane_sb[t][:])
+        nc.vector.tensor_copy(stage[:, 2 * T : 3 * T], plane_sb[2][:])
+        nc.sync.dma_start(rows[2], plane_sb[2][:])
+        nc.scalar.dma_start(rows[3], plane_sb[3][:])
+        thirds = [slice(j * T // 3, (j + 1) * T // 3) for j in range(3)]
+        for cols in thirds:
+            nc.scalar.copy(stage[:, 3 * T : 4 * T][:, cols], plane_sb[3][:, cols])
 
-        def weave_rows(j, copy):
-            fours = slice(j * C1 // 4, (j + 1) * C1 // 4)
+        for cols, copy in zip(thirds, [nc.vector.tensor_copy, nc.vector.tensor_copy, nc.scalar.copy]):
+            runs = slice(cols.start // RUN, cols.stop // RUN)
             copy(
-                fin[:].rearrange("p (c i t) -> p c t i", i=4, t=4)[:, fours],
-                stage[:].rearrange("p (t c i) -> p c t i", i=4, t=4)[:, fours],
+                rounded[:].rearrange("p (c r t) -> p c t r", r=RUN, t=PLANES)[:, runs],
+                stage[:].rearrange("p (t c r) -> p c t r", r=RUN, t=PLANES)[:, runs],
             )
-
-        def hand_on(j):
-            cols = slice(j * C1, (j + 1) * C1)
+        words_out = out_1[0].rearrange("p c d -> p (c d)").bitcast(I32)
+        for cols in thirds:
             nc.vector.quantize_mx(
-                out=ocodes[:, cols].bitcast(FP8X4), scales=oscal[:, cols], in_=fin[:, 4 * j * C1 : 4 * (j + 1) * C1]
+                out=out_codes[:, cols].bitcast(FP8X4),
+                scales=out_scales[:, cols],
+                in_=rounded[:, PLANES * cols.start : PLANES * cols.stop],
             )
-            nc.sync.dma_start(words_out[:, cols], ocodes[:, cols].bitcast(I32))
-
-        weave_rows(0, nc.vector.tensor_copy)
-        weave_rows(1, nc.vector.tensor_copy)
-        weave_rows(2, nc.scalar.copy)
-        for j in range(3):
-            hand_on(j)
-        for q in range(4):
-            nc.scalar.dma_start(out_2[0, 4 * q : 4 * q + 4, :].bitcast(I32), oscal[32 * q : 32 * q + 4, :].bitcast(I32))
+            nc.sync.dma_start(words_out[:, cols], out_codes[:, cols].bitcast(I32))
+        for q in range(QUADRANTS):
+            nc.scalar.dma_start(
+                out_2[0, 4 * q : 4 * q + 4, :].bitcast(I32), out_scales[32 * q : 32 * q + 4, :].bitcast(I32)
+            )

from contextlib import ExitStack

import concourse.mybir as mybir
from concourse.masks import make_identity

K, T, G, C1, E, C2, H, N = 1024, 768, 3, 256, 6, 128, 512, 512
FLOPS = 2 * T * (K * H + H * N)

F32 = mybir.dt.float32
BF16 = mybir.dt.bfloat16
I32 = mybir.dt.int32
U32 = mybir.dt.uint32
U16 = mybir.dt.uint16
U8 = mybir.dt.uint8
FP8X4 = mybir.dt.float8_e4m3fn_x4
FP4X4 = mybir.dt.float4_e2m1fn_x4
COPY = mybir.ActivationFunctionType.Copy
MULT = mybir.AluOpType.mult

P = 128
PASSES = K // 512
PLANES = 4
QUADRANTS = 4
LIST = 16
E2M1_ROW = 2 * N
ACC_BANKS = 3
RUN = 4


def tile_moe_hie_none_kernel(
    tc, x_words, x_scales, wg_words, wg_scales, we_words, we_scales, gate, offs, offs2, dst, out_0, out_1, out_2
):
    nc = tc.nc
    with ExitStack() as ctx:
        keep = ctx.enter_context(tc.tile_pool(name="keep", bufs=1))
        psum = ctx.enter_context(tc.psum_pool(name="psum", bufs=1))

        def held(shape, dtype, name, tag=None):
            return keep.tile(shape, dtype, name=name, tag=tag or name, align_bytes=64)

        offs_sb = held([P, T // LIST], U16, "offs_sb")
        offs2_sb = held([P, T // LIST], U16, "offs2_sb")
        dst_sb = held([P, T // LIST], U16, "dst_sb")
        xw = held([P, PASSES * T], U32, "xw")
        xs = held([P, T], U8, "xs")
        wgw = [held([P, PASSES * H], U32, "wgw%d" % f) for f in range(G)]
        wgs = [held([P, H], U8, "wgs%d" % j) for j in range(2)]
        wew = [held([P, 2 * E2M1_ROW], U8, "wew0"), held([P, 4 * E2M1_ROW], U8, "wew1")]
        wes = held([P, E * N], U8, "wes")
        gate_sb = [held([P, C1], F32, "gate0"), held([P, 2 * C1], F32, "gate1")]
        ident = held([P, P], F32, "ident")
        a_words = [held([P, C1 * max(3, f + 2)], F32, "a_words%d" % f) for f in range(G)]

        nc.gpsimd.memset(xs[:].bitcast(I32), 0)
        nc.vector.memset(wgs[0][:].bitcast(I32), 0)
        zeros = a_words[0][:, 2 * C1 : 3 * C1]
        nc.vector.memset(zeros, 0.0)
        nc.vector.memset(wes[:].bitcast(I32), 0)
        nc.vector.memset(wgs[1][:].bitcast(I32), 0)
        for f in range(1, G):
            for j in range(f):
                nc.scalar.activation(a_words[f][:, j * C1 : (j + 1) * C1], zeros, COPY)
        make_identity(nc, ident[:])

        wg_rows = wg_scales.rearrange("f s b i -> (f s) b i").bitcast(I32)
        we_rows = we_scales.rearrange("e s b n -> (s b) e n").bitcast(I32)

        def load_group_words(f):
            nc.sync.dma_start(
                wgw[f][:].bitcast(I32).rearrange("p (s i) -> p s i", s=PASSES),
                wg_words[f].rearrange("s p i d -> p s (i d)").bitcast(I32),
            )

        def load_expert_words(j, first, count):
            nc.sync.dma_start(
                wew[j][:].bitcast(I32).rearrange("p (e c) -> p e c", e=count),
                we_words[first : first + count].rearrange("e s p c -> p (e s) c").bitcast(I32),
            )

        def load_group_scales(j, first, count):
            for q in range(QUADRANTS):
                nc.sync.dma_start(
                    wgs[j][32 * q : 32 * q + 4 * count, :].bitcast(I32),
                    wg_rows[first : first + count, 4 * q : 4 * q + 4, :],
                )

        nc.sync.dma_start(offs_sb[:], offs)
        nc.sync.dma_start(offs2_sb[:], offs2)
        nc.sync.dma_start(dst_sb[:], dst)
        for q in range(QUADRANTS):
            nc.sync.dma_start(
                xs[32 * q : 32 * q + 4 * PASSES, :].bitcast(I32), x_scales[:, 4 * q : 4 * q + 4, :].bitcast(I32)
            )
        nc.sync.dma_start(
            xw[:].bitcast(I32).rearrange("p (s t) -> p s t", s=PASSES),
            x_words.rearrange("s p t d -> p s (t d)").bitcast(I32),
        )
        load_group_words(0)
        load_group_scales(0, 0, 2 * PASSES)
        load_expert_words(0, 0, 2)
        load_group_words(1)
        load_group_words(2)
        load_group_scales(1, 2 * PASSES, PASSES)
        for q in range(QUADRANTS):
            nc.sync.dma_start(
                wes[32 * q : 32 * q + 4, :].bitcast(I32).rearrange("p (e c) -> p e c", e=E),
                we_rows[4 * q : 4 * q + 4],
            )
        load_expert_words(1, 2, 4)
        nc.sync.dma_start(gate_sb[0][:], gate[:, 0:C1])
        nc.sync.dma_start(gate_sb[1][:], gate[:, C1:T])

        xg = [held([P, T], U32, "xg%d" % s) for s in range(PASSES)]
        xgs = held([P, T], U8, "xgs")
        dealt_words = {}
        dealt_scales = {}
        codes = [held([P, C1], U32, "codes%d" % f) for f in range(G)]
        code_scales = [held([P, C1], U8, "code_scales%d" % f) for f in range(G)]
        results = {}

        def entries(list_sb, lo, n):
            return list_sb[:, lo // LIST : (lo + n) // LIST]

        def gather_scales(lo, n):
            nc.vector.tensor_copy(xgs[:, lo : lo + n], xs[:].indirect(entries(offs_sb, lo, n)))

        def gather_tokens(lo, n):
            for s in range(PASSES):
                window = xw[:, s * T : (s + 1) * T]
                nc.vector.tensor_copy(xg[s][:, lo : lo + n], window.indirect(entries(offs_sb, lo, n)))

        def first_layer(f, h, pairs_tag=None):
            block = 2 * f + h
            cols = slice(block * P, (block + 1) * P)
            acc = psum.tile([P, H], F32, name="acc", tag="acc%d" % (block % ACC_BANKS))
            for s in range(PASSES):
                row = 4 * (PASSES * (f % 2) + s)
                nc.tensor.matmul_mx(
                    out=acc[:],
                    lhsT=xg[s][:, cols].bitcast(FP8X4),
                    lhsT_scale=xgs[4 * s : P, cols],
                    rhs=wgw[f][:, s * H : (s + 1) * H].bitcast(FP8X4),
                    rhs_scale=wgs[f // 2][row:P, :],
                    start=(s == 0),
                    stop=(s == PASSES - 1),
                )
            pairs = held([P, H], BF16, "pairs%d" % block, pairs_tag)
            nc.scalar.copy(
                pairs[:].rearrange("s (u p e) -> s u p e", u=2, e=2),
                acc[:].rearrange("s (p u e) -> s u p e", u=2, e=2),
            )
            turned = psum.tile([P, 2 * P], F32, name="turned", tag="turned%d" % h)
            words = pairs[:].bitcast(F32)
            for u in range(2):
                nc.tensor.transpose(turned[:, u * P : (u + 1) * P], words[:, u * P : (u + 1) * P], ident[:])
            halves = a_words[f][:, f * C1 : (f + 2) * C1].rearrange("p (u c) -> p u c", u=2)
            nc.scalar.copy(halves[:, :, h * P : (h + 1) * P], turned[:].rearrange("p (u c) -> p u c", u=2))

        def deal_expert_words(e, tag=None):
            dealt_words[e] = held([P, E2M1_ROW], U8, "dealt_words%d" % e, tag)
            j, place = (0, e) if e < 2 else (1, e - 2)
            src = wew[j][:, place * E2M1_ROW : (place + 1) * E2M1_ROW].bitcast(U16)
            nc.scalar.copy(
                dealt_words[e][:].bitcast(U16).rearrange("p (t m) -> p t m", t=PLANES),
                src.rearrange("p (m t) -> p t m", t=PLANES),
            )

        def deal_expert_scales(f, tag=None):
            dealt_scales[f] = held([P, 2 * N], U8, "dealt_scales%d" % f, tag)
            nc.vector.tensor_copy(
                dealt_scales[f][:].rearrange("p (e t m) -> p e t m", e=2, t=PLANES),
                wes[:, 2 * f * N : (2 * f + 2) * N].rearrange("p (e m t) -> p e t m", e=2, t=PLANES),
            )

        def regroup(f, lo, n, picked_tag=None, woven_tag=None):
            width = C1 * max(2, f + 1)
            picked = held([P, 2 * n], U32, "picked%d_%d" % (f, lo), picked_tag)
            for u in range(2):
                window = a_words[f][:, u * C1 : u * C1 + width].bitcast(U32)
                nc.vector.tensor_copy(
                    picked[:, u * n : (u + 1) * n], window.indirect(entries(offs2_sb, f * C1 + lo, n))
                )
            woven = held([P, 4 * n], BF16, "woven%d_%d" % (f, lo), woven_tag)
            nc.vector.tensor_copy(
                woven[:].bitcast(I32).rearrange("p (c r u) -> p c u r", r=RUN, u=2),
                picked[:].bitcast(I32).rearrange("p (u c r) -> p c u r", r=RUN, u=2),
            )
            return woven

        def quantize(f, lo, n, woven):
            cols = slice(lo, lo + n)
            nc.vector.quantize_mx(out=codes[f][:, cols].bitcast(FP8X4), scales=code_scales[f][:, cols], in_=woven[:])

        def second_layer(f, planes, experts, tag):
            bank = psum.tile([P, len(planes), len(experts), C2], F32, name="bank", tag=tag)
            for j, t in enumerate(planes):
                for place, h in enumerate(experts):
                    nc.tensor.matmul_mx(
                        out=bank[:, j, place, :],
                        lhsT=dealt_words[2 * f + h][:, t * 2 * P : (t + 1) * 2 * P].bitcast(FP4X4),
                        lhsT_scale=dealt_scales[f][:, h * N + t * P : h * N + (t + 1) * P],
                        rhs=codes[f][:, h * C2 : (h + 1) * C2].bitcast(FP8X4),
                        rhs_scale=code_scales[f][:, h * C2 : (h + 1) * C2],
                        start=True,
                        stop=True,
                    )
            return bank

        def weigh(f, planes, experts, bank, tag=None):
            lo, n = experts[0] * C2, len(experts) * C2
            weighed = held([P, len(planes) * n], F32, "weighed%d_%d_%d" % (f, planes[0], experts[0]), tag)
            first = lo if f == 0 else (f - 1) * C1 + lo
            weights = gate_sb[min(f, 1)][:, first : first + n]
            nc.vector.tensor_tensor(
                weighed[:].rearrange("p (t c) -> p t c", c=n),
                bank[:].rearrange("p t h c -> p t (h c)"),
                weights.unsqueeze(1).to_broadcast([P, len(planes), n]),
                MULT,
            )
            for j, t in enumerate(planes):
                for place, h in enumerate(experts):
                    results[f, t, h] = (weighed, j * n + place * C2)

        def scatter(on_vector, f, t, h=0, n=C1):
            weighed, lo = results[f, t, h]
            window = plane_sb[t][:].indirect(entries(dst_sb, f * C1 + h * C2, n))
            if on_vector:
                nc.vector.tensor_copy(window, weighed[:, lo : lo + n])
            else:
                nc.scalar.activation(window, weighed[:, lo : lo + n], COPY)

        deal_expert_words(0)
        deal_expert_words(1)
        gather_scales(0, T // 2)
        gather_tokens(0, P)
        first_layer(0, 0, "wew0")
        gather_tokens(P, P)
        first_layer(0, 1)
        gather_scales(T // 2, T // 2)
        for f in range(1, G):
            gather_tokens(f * C1, C1)
            first_layer(f, 0)
            first_layer(f, 1)
        for e, tag in zip(range(2, E), ["pairs3", "pairs4", "xg0", "pairs5"]):
            deal_expert_words(e, tag)

        every_plane, low_planes, high_planes, both = (0, 1, 2, 3), (0, 1), (2, 3), (0, 1)
        deal_expert_scales(0)
        quantize(0, 0, C2, regroup(0, 0, C2))
        sums_e0 = second_layer(0, every_plane, (0,), "acc%d" % ((2 * G - 1) % ACC_BANKS))
        woven = regroup(0, C2, C2)
        deal_expert_scales(1, "picked0_%d" % C2)
        quantize(0, C2, C2, woven)
        sums_e1 = second_layer(0, every_plane, (1,), "bank1")
        weigh(0, every_plane, (0,), sums_e0)
        weigh(0, every_plane, (1,), sums_e1)
        woven = regroup(1, 0, C1, None, "gate0")
        deal_expert_scales(2, "picked1_0")
        quantize(1, 0, C1, woven)
        low_1 = second_layer(1, low_planes, both, "bank2")
        high_1 = second_layer(1, high_planes, both, "acc0")
        weigh(1, low_planes, both, low_1)
        quantize(2, 0, C1, regroup(2, 0, C1, "gate0"))
        high_2 = second_layer(2, high_planes, both, "bank0")
        low_2 = second_layer(2, low_planes, both, "bank1")
        weigh(1, high_planes, both, high_1, "woven2_0")
        weigh(2, high_planes, both, high_2)
        weigh(2, low_planes, both, low_2)

        plane_sb = [held([P, T], F32, "plane_sb%d" % t) for t in range(PLANES)]
        for h in range(2):
            for t in range(PLANES):
                scatter(False, 0, t, h, C2)
        for f, t in [(1, 0), (1, 1), (1, 3), (2, 3)]:
            scatter(False, f, t)
        for f, t in [(2, 2), (2, 0), (2, 1), (1, 2)]:
            scatter(True, f, t)

        rows = out_0.rearrange("(p t) c -> t p c", t=PLANES)
        stage = held([P, PLANES * T], F32, "stage")
        rounded = held([P, PLANES * T], BF16, "rounded")
        out_codes = held([P, T], U32, "out_codes")
        out_scales = held([P, T], U8, "out_scales")
        for t in low_planes:
            nc.sync.dma_start(stage[:, t * T : (t + 1) * T], plane_sb[t][:])
            nc.sync.dma_start(rows[t], plane_sb[t][:])
        nc.vector.tensor_copy(stage[:, 2 * T : 3 * T], plane_sb[2][:])
        nc.sync.dma_start(rows[2], plane_sb[2][:])
        nc.scalar.dma_start(rows[3], plane_sb[3][:])
        thirds = [slice(j * T // 3, (j + 1) * T // 3) for j in range(3)]
        for cols in thirds:
            nc.scalar.copy(stage[:, 3 * T : 4 * T][:, cols], plane_sb[3][:, cols])

        for cols, copy in zip(thirds, [nc.vector.tensor_copy, nc.vector.tensor_copy, nc.scalar.copy]):
            runs = slice(cols.start // RUN, cols.stop // RUN)
            copy(
                rounded[:].rearrange("p (c r t) -> p c t r", r=RUN, t=PLANES)[:, runs],
                stage[:].rearrange("p (t c r) -> p c t r", r=RUN, t=PLANES)[:, runs],
            )
        words_out = out_1[0].rearrange("p c d -> p (c d)").bitcast(I32)
        for cols in thirds:
            nc.vector.quantize_mx(
                out=out_codes[:, cols].bitcast(FP8X4),
                scales=out_scales[:, cols],
                in_=rounded[:, PLANES * cols.start : PLANES * cols.stop],
            )
            nc.sync.dma_start(words_out[:, cols], out_codes[:, cols].bitcast(I32))
        for q in range(QUADRANTS):
            nc.scalar.dma_start(
                out_2[0, 4 * q : 4 * q + 4, :].bitcast(I32), out_scales[32 * q : 32 * q + 4, :].bitcast(I32)
            )
